import numpy as np
import ml_dtypes


def mxq(x, axis, fmt="e4m3"):
    dtype, down = {"e4m3": (ml_dtypes.float8_e4m3fn, 7), "e5m2": (ml_dtypes.float8_e5m2, 14)}[fmt]
    v = np.moveaxis(np.asarray(x, np.float32).astype(ml_dtypes.bfloat16).astype(np.float64), axis, -1)
    blocks = v.reshape(v.shape[:-1] + (-1, 32))
    amax = np.abs(blocks).max(-1, keepdims=True)
    byte = np.maximum(np.where(amax > 0, np.frexp(amax)[1] - 1 + 127, 0) - down, 1)
    scale = np.exp2(byte - 127.0)
    codes = (blocks / scale).astype(np.float32).astype(dtype).astype(np.float64)
    return np.moveaxis((codes * scale).reshape(v.shape), -1, axis)


WIDE = False


def mx_kscale(k):
    if not WIDE:
        return np.ones(k)
    levels = np.array([30, -30])
    if k % 512:
        return np.exp2(np.random.permutation(np.resize(levels, k // 32))).repeat(32)
    a = np.empty((k // 512, 16))
    for p in range(k // 512):
        a[p, :8] = np.random.permutation(np.resize(levels, 8))
        for g in range(8):
            far = levels[np.abs(levels - a[p, g]) >= 10]
            a[p, g + 8] = far[np.random.randint(len(far))]
    return np.exp2(a.ravel()).repeat(32)


BF16 = ml_dtypes.bfloat16


def bf(x):
    return np.asarray(x, np.float32).astype(BF16)


def f64(x):
    return np.asarray(x).astype(np.float64)


E2M1 = np.array([0.0, 0.5, 1.0, 1.5, 2.0, 3.0, 4.0, 6.0, -0.0, -0.5, -1.0, -1.5, -2.0, -3.0, -4.0, -6.0])


def pack_weight(w, fmt):
    k, n = w.shape
    w = f64(bf(w)).reshape(k // 32, 32, n)
    amax = np.abs(w).max(1)
    if fmt == "e4m3":
        byte = np.frexp(amax)[1] - 1 + 127 - 7
    else:
        mant, ex = np.frexp(amax / 6.0)
        byte = np.where(mant > 0.5, ex, ex - 1) + 127
    byte = np.clip(np.where(amax > 0, byte, 1), 1, 254)
    scaled = (w * np.exp2(127.0 - byte)[:, None, :]).reshape(k, n).astype(np.float32)
    by_word = np.ascontiguousarray(scaled.reshape(k // 512, 128, 4, n).transpose(0, 1, 3, 2))
    if fmt == "e4m3":
        words = by_word.astype(ml_dtypes.float8_e4m3fn).view(np.uint8)
    else:
        c = by_word.astype(ml_dtypes.float4_e2m1fn).view(np.uint8) & 0xF
        words = c[..., 0::2] | (c[..., 1::2] << 4)
    return np.ascontiguousarray(words), np.ascontiguousarray(byte.astype(np.uint8).reshape(k // 512, 16, n))


def unpack_weight(words, scales, fmt):
    g, p, n, _ = words.shape
    if fmt == "e4m3":
        vals = np.ascontiguousarray(words).view(ml_dtypes.float8_e4m3fn).astype(np.float64)
    else:
        nib = np.empty((g, p, n, 4), np.uint8)
        nib[..., 0::2] = words & 0xF
        nib[..., 1::2] = words >> 4
        vals = E2M1[nib]
    vals = vals * np.repeat(np.exp2(scales.astype(np.float64) - 127.0), 8, axis=1)[..., None]
    return vals.transpose(0, 1, 3, 2).reshape(g * 512, n)
def pack4(w):
    words, scales = pack_weight(w, "e2m1")
    return words.reshape(words.shape[0], 128, -1), scales


def unpack4(words, scales):
    return unpack_weight(words.reshape(words.shape[0], 128, -1, 2), scales, "e2m1")


U, T, D, F = 4, 384, 1536, 1024


def setup_inputs():
    s = mx_kscale(D)
    t = mx_kscale(F)
    x = np.random.standard_normal((U * T, D)) * s
    lda = np.random.standard_normal((D, F)) / np.sqrt(D) / s[:, None]
    lda_words, lda_scales = pack4(lda)
    mean = 0.5 * np.random.standard_normal((U, F))
    inv_std = np.exp(0.5 * np.random.standard_normal((U, F))) * t
    a = np.random.standard_normal((U, F, F)) / np.sqrt(F) / t[:, None]
    b = 0.5 * np.random.standard_normal((U, F))
    return {"x": bf(x), "lda_words": lda_words, "lda_scales": lda_scales,
            "mean": bf(mean), "inv_std": bf(inv_std), "a": bf(a), "b": bf(b)}


def reference(x, lda_words, lda_scales, mean, inv_std, a, b):
    h = mxq(f64(x), 1, "e4m3") @ unpack4(lda_words, lda_scales)
    h = h.reshape(U, T, F)
    z = (h - f64(mean)[:, None, :]) * f64(inv_std)[:, None, :]
    y = mxq(z, 2, "e5m2") @ mxq(f64(a), 1, "e4m3")
    return y + f64(b)[:, None, :]

@@ -1,0 +1,368 @@
+from contextlib import ExitStack
+
+import concourse.mybir as mybir
+from concourse.masks import make_identity
+
+U, T, D, F = 4, 384, 1536, 1024
+FLOPS = 2 * U * T * D * F + 2 * U * T * F * F
+
+F32 = mybir.dt.float32
+BF16 = mybir.dt.bfloat16
+I32 = mybir.dt.int32
+U32 = mybir.dt.uint32
+U8 = mybir.dt.uint8
+E4M3 = mybir.dt.float8_e4m3fn_x4
+E5M2 = mybir.dt.float8_e5m2_x4
+E2M1 = mybir.dt.float4_e2m1fn_x4
+ALU = mybir.AluOpType
+ACT = mybir.ActivationFunctionType
+
+P = 128
+PACK = 4
+KP = P * PACK
+NB = 512
+D_PASSES = D // KP
+F_PASSES = F // KP
+TOKENS = U * T
+GROUPS = TOKENS // NB
+TILES = TOKENS // P
+HALVES = F // NB
+PIECE = 256
+PIECES = U * F_PASSES * (F // PIECE)
+
+
+WARM_PASSES = 5
+TURN_SLOTS = (5, 6, 11, 12)
+VECTOR_WEAVES_UNTIL = 16
+SCALAR_WEAVES_FROM = 11
+ADAPT_FROM, ADAPT_TWICE_FROM = 14, 18
+RAW_A_BUFS = 5
+LOADS = "m x0 x1 s l0 a00 l1 a01 x2 x3 a10 a11 x4 b0 x5 a20 b1 a21 b2 a30 a31 b3"
+
+
+def half_of(n):
+    u, rest = divmod(n, 4)
+    first, second = divmod(rest, 2)
+    return (u, first, second) if u < 2 else (u, second, first)
+
+
+def tile_fmllr_speaker_adaptation_s9_kernel(tc, x, lda_words, lda_scales, mean, inv_std, a, b, out):
+    nc = tc.nc
+    out_rows = out.rearrange("u t f -> (u t) f")
+
+    with ExitStack() as ctx:
+        keep = ctx.enter_context(tc.tile_pool(name="keep", bufs=1))
+        work = ctx.enter_context(tc.tile_pool(name="work", bufs=2))
+        psum = ctx.enter_context(tc.psum_pool(name="psum", bufs=1))
+        ctx.enter_context(tc.manual_schedule())
+
+        ident = keep.tile([P, P], F32, name="ident")
+        stat_rows = keep.tile([16, KP], BF16, name="stat_rows")
+        stat_sorted = keep.tile([P, PACK, P], F32, name="stat_sorted")
+        stat_cols = keep.tile([P, PACK, 16], F32, name="stat_cols")
+        shift = keep.tile([P, PACK, 8], F32, name="shift")
+        l_scales_raw = keep.tile([P, D_PASSES * F], U8, name="l_scales_raw", align_bytes=64)
+        l_scales = keep.tile([P, D_PASSES * F], U8, name="l_scales", align_bytes=64)
+        l_raw, l_codes = {}, {}
+        x_raw, x_grouped, x_codes, x_scales = {}, {}, {}, {}
+        a_raw, a_grouped, a_codes, a_scales = {}, {}, {}, {}
+        z_raw, z_grouped, z_codes, z_scales = {}, {}, {}, {}
+        b_rows, y_tiles, x_banks, h_banks, y_banks = {}, {}, {}, {}, {}
+
+        def load_x(pair):
+            x_raw[pair] = work.tile([P, 2, D], BF16, name="x_raw", bufs=4)
+            nc.sync.dma_start(out=x_raw[pair][:], in_=x[2 * P * pair : 2 * P * (pair + 1), :].rearrange("(i p) d -> p i d", p=P))
+
+        def load_l(g):
+            l_raw[g] = keep.tile([P, D_PASSES, F], U8, name="l_raw%d" % g, align_bytes=64)
+            words = lda_words.bitcast(I32).rearrange("c p (g w) -> g p c w", g=F_PASSES)
+            nc.sync.dma_start(out=l_raw[g][:].bitcast(I32), in_=words[g])
+
+        def load_l_scales():
+            nc.vector.memset(l_scales_raw[:].bitcast(I32), 0)
+            rows = lda_scales.bitcast(I32)
+            for q in range(4):
+                nc.sync.dma_start(
+                    out=l_scales_raw[32 * q : 32 * q + 4, :].bitcast(I32).rearrange("r (c w) -> r c w", c=D_PASSES),
+                    in_=rows[:, 4 * q : 4 * q + 4, :].rearrange("c r w -> r c w"),
+                )
+
+        def load_stats():
+            nc.sync.dma_start(out=stat_rows[0:8, :], in_=mean.rearrange("u (g k) -> (u g) k", k=KP))
+            nc.sync.dma_start(out=stat_rows[8:16, :], in_=inv_std.rearrange("u (g k) -> (u g) k", k=KP))
+
+        def load_a(u, g):
+            a_raw[u, g] = work.tile([P, PACK, F], BF16, name="a_raw", bufs=RAW_A_BUFS)
+            rows = a[u, KP * g : KP * (g + 1), :].rearrange("(j t i) n -> i j t n", t=PACK, i=4)
+            for i in range(4):
+                nc.sync.dma_start(out=a_raw[u, g][i:P:4, :, :], in_=rows[i])
+
+        def load_b(u):
+            b_rows[u] = keep.tile([P, F], BF16, name="b_rows%d" % u)
+            nc.sync.dma_start(out=b_rows[u][:], in_=b[u].partition_broadcast(P))
+
+        def sort_l(g):
+            l_codes[g] = keep.tile([P, D_PASSES, F], U8, name="l_codes%d" % g, align_bytes=64)
+            nc.vector.tensor_copy(
+                out=l_codes[g][:].bitcast(I32).rearrange("p c (t j w) -> p c t j w", t=PACK, w=2),
+                in_=l_raw[g][:].bitcast(I32).rearrange("p c (j t w) -> p c t j w", t=PACK, w=2),
+            )
+
+        def sort_l_scales():
+            nc.vector.tensor_copy(
+                out=l_scales[:].bitcast(I32).rearrange("p (m t j) -> p m t j", t=PACK, j=32),
+                in_=l_scales_raw[:].bitcast(I32).rearrange("p (m j t) -> p m t j", t=PACK, j=32),
+            )
+
+        def sort_stats():
+            nc.vector.memset(stat_sorted[:], 0.0)
+            nc.vector.tensor_copy(
+                out=stat_sorted[0:16, :, :].rearrange("r t (j i) -> r t j i", i=4),
+                in_=stat_rows[:].rearrange("r (j t i) -> r t j i", t=PACK, i=4),
+            )
+
+        def turn_stats():
+            bank = psum.tile([P, PACK, P], F32, name="bank", bufs=8)
+            for t in range(PACK):
+                nc.tensor.transpose(bank[:, t, :], stat_sorted[:, t, :], ident[:])
+            nc.scalar.activation(out=stat_cols[:], in_=bank[:, :, 0:16], func=ACT.Identity)
+            nc.vector.scalar_tensor_tensor(
+                out=shift[:], in0=stat_cols[:, :, 0:8], scalar=-1.0, in1=stat_cols[:, :, 8:16], op0=ALU.mult, op1=ALU.mult
+            )
+
+        def turn_x(pair, c):
+            x_banks[pair, c] = psum.tile([P, 2, 2, P], F32, name="bank", bufs=8)
+            for i in range(2):
+                words = x_raw[pair][:, i, :].bitcast(F32)
+                for e in range(2):
+                    nc.tensor.transpose(x_banks[pair, c][:, i, e, :], words[:, 256 * c + e : 256 * (c + 1) : 2], ident[:])
+
+        def copy_x(pair, c):
+            grp, half = divmod(pair, 2)
+            if half == 0:
+                x_grouped[grp, c] = work.tile([P, NB * PACK], BF16, name="x_grouped", bufs=4, align_bytes=64)
+            dst = x_grouped[grp, c][:, half * 2 * P * PACK : (half + 1) * 2 * P * PACK].bitcast(F32)
+            nc.scalar.copy(
+                out=dst.rearrange("p (i r e) -> p i r e", i=2, e=2),
+                in_=x_banks[pair, c][:].rearrange("p i e r -> p i r e"),
+            )
+
+        def quant_x(grp, c):
+            x_codes[grp, c] = work.tile([P, NB], U32, name="x_codes", bufs=6, align_bytes=64)
+            x_scales[grp, c] = work.tile([P, NB], U8, name="x_scales", bufs=6, align_bytes=64)
+            nc.vector.quantize_mx(out=x_codes[grp, c][:].bitcast(E4M3), scales=x_scales[grp, c][:], in_=x_grouped[grp, c][:])
+
+        def weave(engine_copy, dst, src):
+            engine_copy(
+                out=dst.rearrange("p (c i t) -> p c t i", i=4, t=PACK),
+                in_=src.rearrange("p t (c i) -> p c t i", i=4),
+            )
+
+        def weave_a(piece, engine_copy):
+            half, part = divmod(piece, 2)
+            u, g, h = half_of(half)
+            if part == 0:
+                a_grouped[half] = work.tile([P, NB * PACK], BF16, name="a_grouped", bufs=4, align_bytes=64)
+            col = NB * h + PIECE * part
+            weave(
+                engine_copy,
+                a_grouped[half][:, PIECE * PACK * part : PIECE * PACK * (part + 1)],
+                a_raw[u, g][:, :, col : col + PIECE],
+            )
+
+        def quant_a(half):
+            a_codes[half] = work.tile([P, NB], U32, name="a_codes", bufs=12, align_bytes=64)
+            a_scales[half] = work.tile([P, NB], U8, name="a_scales", bufs=12, align_bytes=64)
+            nc.vector.quantize_mx(out=a_codes[half][:].bitcast(E4M3), scales=a_scales[half][:], in_=a_grouped[half][:])
+
+        def project(slot):
+            grp, g, t = slot // 8, slot // 4 % 2, slot % 4
+            h_banks[slot] = psum.tile([P, NB], F32, name="bank", bufs=8)
+            m = (g * PACK + t) * P
+            for c in range(D_PASSES):
+                nc.tensor.matmul_mx(
+                    out=h_banks[slot][:],
+                    lhsT=l_codes[g][:, c, 2 * P * t : 2 * P * (t + 1)].bitcast(E2M1),
+                    lhsT_scale=l_scales[:, c * F + m : c * F + m + P],
+                    rhs=x_codes[grp, c][:].bitcast(E4M3),
+                    rhs_scale=x_scales[grp, c][:],
+                    start=(c == 0),
+                    stop=(c == D_PASSES - 1),
+                )
+
+        def normalise(slot):
+            grp, g, t = slot // 8, slot // 4 % 2, slot % 4
+            if t == 0:
+                z_raw[grp, g] = work.tile([P, PACK, NB], BF16, name="z_raw", bufs=2)
+            first = NB * grp
+            cut = (first // T + 1) * T
+            for lo, hi in ((first, cut), (cut, first + NB)):
+                row = (lo // T) * F_PASSES + g
+                nc.scalar.activation(
+                    out=z_raw[grp, g][:, t, lo - first : hi - first],
+                    in_=h_banks[slot][:, lo - first : hi - first],
+                    func=ACT.Identity,
+                    bias=shift[:, t, row : row + 1],
+                    scale=stat_cols[:, t, 8 + row : 8 + row + 1],
+                )
+
+        def weave_z(grp, g):
+            z_grouped[grp, g] = work.tile([P, NB * PACK], BF16, name="z_grouped", bufs=2, align_bytes=64)
+            weave(nc.vector.tensor_copy, z_grouped[grp, g][:], z_raw[grp, g][:])
+
+        def quant_z(grp, g):
+            z_codes[grp, g] = work.tile([P, NB], U32, name="z_codes", bufs=4, align_bytes=64)
+            z_scales[grp, g] = work.tile([P, NB], U8, name="z_scales", bufs=4, align_bytes=64)
+            nc.vector.quantize_mx(out=z_codes[grp, g][:].bitcast(E5M2), scales=z_scales[grp, g][:], in_=z_grouped[grp, g][:])
+
+        def adapt(k):
+            tile, h = divmod(k, HALVES)
+            grp, i = divmod(tile, 4)
+            u = tile * P // T
+            y_banks[k] = psum.tile([P, NB], F32, name="bank", bufs=8)
+            for g in range(F_PASSES):
+                half = [half_of(n) for n in range(16)].index((u, g, h))
+                nc.tensor.matmul_mx(
+                    out=y_banks[k][:],
+                    lhsT=z_codes[grp, g][:, P * i : P * (i + 1)].bitcast(E5M2),
+                    lhsT_scale=z_scales[grp, g][:, P * i : P * (i + 1)],
+                    rhs=a_codes[half][:].bitcast(E4M3),
+                    rhs_scale=a_scales[half][:],
+                    start=(g == 0),
+                    stop=(g == F_PASSES - 1),
+                )
+
+        def add_bias(k):
+            tile, h = divmod(k, HALVES)
+            u = tile * P // T
+            if h == 0:
+                y_tiles[tile] = work.tile([P, F], F32, name="y_tile", bufs=6)
+            nc.vector.tensor_tensor(out=y_tiles[tile][:, NB * h : NB * (h + 1)], in0=y_banks[k][:], in1=b_rows[u][:, NB * h : NB * (h + 1)], op=ALU.add)
+
+        def store(k):
+            tile, h = divmod(k, HALVES)
+            if tile >= 8:
+                nc.sync.dma_start(out=out_rows[P * tile : P * (tile + 1), NB * h : NB * (h + 1)], in_=y_tiles[tile][:, NB * h : NB * (h + 1)])
+            elif h == 1:
+                nc.sync.dma_start(out=out_rows[P * tile : P * (tile + 1), :], in_=y_tiles[tile][:])
+
+        def warm_operands():
+            zeros = keep.tile([P, NB * PACK], BF16, name="zeros", align_bytes=64)
+            nc.vector.memset(zeros[:].bitcast(I32), 0)
+            for name, cols, fmt in (("w4", NB, E4M3), ("w5", P, E5M2)):
+                a_codes[name] = keep.tile([P, cols], U32, name=name + "c", align_bytes=64)
+                a_scales[name] = keep.tile([P, cols], U8, name=name + "s", align_bytes=64)
+                nc.vector.quantize_mx(out=a_codes[name][:].bitcast(fmt), scales=a_scales[name][:], in_=zeros[:, : cols * PACK])
+
+        def warm(n):
+            bank = psum.tile([P, NB], F32, name="bank", bufs=8)
+            for k in range(n):
+                nc.tensor.matmul_mx(out=bank[:], lhsT=a_codes["w5"][:].bitcast(E5M2), lhsT_scale=a_scales["w5"][:],
+                                    rhs=a_codes["w4"][:].bitcast(E4M3), rhs_scale=a_scales["w4"][:], start=True, stop=True)
+
+        waiting = LOADS.split()
+        count = {"woven": 0, "quantised": 0, "adapted": 0, "added": 0, "stored": 0}
+        bank_order = list(range(18)) + [18, 20, 22, 19, 21, 23]
+
+        def loads():
+            while waiting:
+                item = waiting[0]
+                if item[0] == "a":
+                    old = 2 * int(item[1]) + int(item[2]) - RAW_A_BUFS
+                    done = [half_of(n)[:2] for n in range(count["woven"] // 2)]
+                    if old >= 0 and done.count(divmod(old, 2)) < 2:
+                        return
+                    load_a(int(item[1]), int(item[2]))
+                elif item[0] == "x":
+                    if int(item[1]) >= 4 and (int(item[1]) - 4, 2) not in x_banks:
+                        return
+                    load_x(int(item[1]))
+                elif item[0] == "l":
+                    load_l(int(item[1]))
+                elif item == "m":
+                    load_stats()
+                elif item == "s":
+                    load_l_scales()
+                else:
+                    load_b(int(item[1]))
+                waiting.remove(item)
+
+        def weave_next(engine_copy):
+            weave_a(count["woven"], engine_copy)
+            count["woven"] = count["woven"] + 1
+            loads()
+
+        def quantise_until(pieces):
+            while count["quantised"] < pieces // 2:
+                quant_a(count["quantised"])
+                count["quantised"] = count["quantised"] + 1
+
+        def adapt_next():
+            adapt(bank_order[count["adapted"]])
+            count["adapted"] = count["adapted"] + 1
+
+        def add_until(n):
+            while count["added"] < n:
+                add_bias(bank_order[count["added"]])
+                count["added"] = count["added"] + 1
+            while not waiting and count["stored"] < count["added"]:
+                store(bank_order[count["stored"]])
+                count["stored"] = count["stored"] + 1
+
+        def turn_pair(pair):
+            for c in range(D_PASSES):
+                turn_x(pair, c)
+                copy_x(pair, c)
+            loads()
+
+        make_identity(nc, ident[:])
+        loads()
+        warm_operands()
+        warm(WARM_PASSES)
+        sort_stats()
+        turn_stats()
+        turn_pair(0)
+        turn_pair(1)
+        sort_l_scales()
+        sort_l(0)
+        for c in range(D_PASSES):
+            quant_x(0, c)
+
+        for slot in range(24):
+            woven = count["woven"]
+            project(slot)
+            if slot == 2:
+                sort_l(1)
+            normalise(slot)
+            if slot >= SCALAR_WEAVES_FROM and slot - 1 not in TURN_SLOTS:
+                weave_next(nc.scalar.copy)
+            if slot > 4 and slot % 4 == 1:
+                weave_z(*divmod(slot // 4 - 1, 2))
+            add_until(count["adapted"] - 1)
+            quantise_until(woven)
+            if slot < VECTOR_WEAVES_UNTIL:
+                weave_next(nc.vector.tensor_copy)
+            if slot > 4 and slot % 4 == 1:
+                quant_z(*divmod(slot // 4 - 1, 2))
+            if slot - 1 in TURN_SLOTS[1::2]:
+                for c in range(D_PASSES):
+                    quant_x(slot // 8 + 1, c)
+            for k in range((slot >= ADAPT_FROM) + (slot >= ADAPT_TWICE_FROM)):
+                adapt_next()
+            if slot in TURN_SLOTS:
+                turn_pair(2 + TURN_SLOTS.index(slot))
+
+        weave_z(2, 1)
+        quantise_until(count["woven"])
+        add_until(count["added"] + 1)
+        quant_z(2, 1)
+        add_until(count["adapted"])
+        while count["adapted"] < 24:
+            tile, h = divmod(bank_order[count["adapted"]], HALVES)
+            need = 2 * (4 * (tile * P // T) + 2 * h + 2)
+            while count["woven"] < need:
+                weave_next(nc.scalar.copy)
+            quantise_until(need)
+            adapt_next()
+            add_until(count["adapted"] - 1)
+        add_until(24)

@@ -31,19 +31,25 @@ PIECE = 256
 PIECES = U * F_PASSES * (F // PIECE)
 
 
-WARM_PASSES = 5
-TURN_SLOTS = (5, 6, 11, 12)
-VECTOR_WEAVES_UNTIL = 16
-SCALAR_WEAVES_FROM = 11
-ADAPT_FROM, ADAPT_TWICE_FROM = 14, 18
+WARM_FIRST, WARM_AGAIN = 3, 2
+TURN_SLOTS = (3, 5, 8, 10)
+VECTOR_WEAVES_UNTIL = 13
+ADAPT_FROM = 16
+BURST = 4
+POOL_COLUMNS = 384
+POOL_HALVES = (9, 11, 13, 14, 15)
 RAW_A_BUFS = 5
-LOADS = "m x0 x1 s l0 a00 l1 a01 x2 x3 a10 a11 x4 b0 x5 a20 b1 a21 b2 a30 a31 b3"
+LOADS = "m x0 x1 s l0 a00 l1 x2 a01 x3 a10 x4 a11 x5 a20 b a21 a30 a31"
 
 
 def half_of(n):
     u, rest = divmod(n, 4)
     first, second = divmod(rest, 2)
     return (u, first, second) if u < 2 else (u, second, first)
+
+
+def half_index(u, g, h):
+    return 4 * u + (2 * g + h if u < 2 else 2 * h + g)
 
 
 def tile_fmllr_speaker_adaptation_s9_kernel(tc, x, lda_words, lda_scales, mean, inv_std, a, b, out):
@@ -67,7 +73,9 @@ def tile_fmllr_speaker_adaptation_s9_kernel(tc, x, lda_words, lda_scales, mean, 
         x_raw, x_grouped, x_codes, x_scales = {}, {}, {}, {}
         a_raw, a_grouped, a_codes, a_scales = {}, {}, {}, {}
         z_raw, z_grouped, z_codes, z_scales = {}, {}, {}, {}
-        b_rows, y_tiles, x_banks, h_banks, y_banks = {}, {}, {}, {}, {}
+        woven = []
+        y_tiles, x_banks, h_banks, y_banks = {}, {}, {}, {}
+        b_rows = keep.tile([P, U * F], BF16, name="b_rows")
 
         def load_x(pair):
             x_raw[pair] = work.tile([P, 2, D], BF16, name="x_raw", bufs=4)
@@ -97,9 +105,8 @@ def tile_fmllr_speaker_adaptation_s9_kernel(tc, x, lda_words, lda_scales, mean, 
             for i in range(4):
                 nc.sync.dma_start(out=a_raw[u, g][i:P:4, :, :], in_=rows[i])
 
-        def load_b(u):
-            b_rows[u] = keep.tile([P, F], BF16, name="b_rows%d" % u)
-            nc.sync.dma_start(out=b_rows[u][:], in_=b[u].partition_broadcast(P))
+        def load_b():
+            nc.sync.dma_start(out=b_rows[:], in_=b.rearrange("u f -> (u f)").partition_broadcast(P))
 
         def sort_l(g):
             l_codes[g] = keep.tile([P, D_PASSES, F], U8, name="l_codes%d" % g, align_bytes=64)
@@ -158,17 +165,18 @@ def tile_fmllr_speaker_adaptation_s9_kernel(tc, x, lda_words, lda_scales, mean, 
                 in_=src.rearrange("p t (c i) -> p c t i", i=4),
             )
 
-        def weave_a(piece, engine_copy):
-            half, part = divmod(piece, 2)
+        def pool_copy(out, in_):
+            nc.gpsimd.tensor_scalar(out=out, in0=in_, scalar1=1.0, scalar2=0.0, op0=ALU.mult, op1=ALU.add)
+
+        def weave_a(half, lo, hi, engine_copy):
             u, g, h = half_of(half)
-            if part == 0:
+            if lo == 0 and half in POOL_HALVES:
+                a_grouped[half] = work.tile([P, NB * PACK], BF16, name="gated", bufs=1, align_bytes=64)
+            elif lo == 0:
                 a_grouped[half] = work.tile([P, NB * PACK], BF16, name="a_grouped", bufs=4, align_bytes=64)
-            col = NB * h + PIECE * part
-            weave(
-                engine_copy,
-                a_grouped[half][:, PIECE * PACK * part : PIECE * PACK * (part + 1)],
-                a_raw[u, g][:, :, col : col + PIECE],
-            )
+            weave(engine_copy, a_grouped[half][:, PACK * lo : PACK * hi], a_raw[u, g][:, :, NB * h + lo : NB * h + hi])
+            if hi == NB:
+                woven.append(half)
 
         def quant_a(half):
             a_codes[half] = work.tile([P, NB], U32, name="a_codes", bufs=12, align_bytes=64)
@@ -206,38 +214,40 @@ def tile_fmllr_speaker_adaptation_s9_kernel(tc, x, lda_words, lda_scales, mean, 
                     scale=stat_cols[:, t, 8 + row : 8 + row + 1],
                 )
 
-        def weave_z(grp, g):
-            z_grouped[grp, g] = work.tile([P, NB * PACK], BF16, name="z_grouped", bufs=2, align_bytes=64)
-            weave(nc.vector.tensor_copy, z_grouped[grp, g][:], z_raw[grp, g][:])
+        def weave_z(grp, g, engine_copy):
+            if (grp, g) == (1, 1):
+                z_grouped[grp, g] = work.tile([P, NB * PACK], BF16, name="gated", bufs=1, align_bytes=64)
+            else:
+                z_grouped[grp, g] = work.tile([P, NB * PACK], BF16, name="z_grouped", bufs=2, align_bytes=64)
+            weave(engine_copy, z_grouped[grp, g][:], z_raw[grp, g][:])
 
         def quant_z(grp, g):
             z_codes[grp, g] = work.tile([P, NB], U32, name="z_codes", bufs=4, align_bytes=64)
             z_scales[grp, g] = work.tile([P, NB], U8, name="z_scales", bufs=4, align_bytes=64)
             nc.vector.quantize_mx(out=z_codes[grp, g][:].bitcast(E5M2), scales=z_scales[grp, g][:], in_=z_grouped[grp, g][:])
 
-        def adapt(k):
+        def adapt(k, g):
             tile, h = divmod(k, HALVES)
             grp, i = divmod(tile, 4)
-            u = tile * P // T
-            y_banks[k] = psum.tile([P, NB], F32, name="bank", bufs=8)
-            for g in range(F_PASSES):
-                half = [half_of(n) for n in range(16)].index((u, g, h))
-                nc.tensor.matmul_mx(
-                    out=y_banks[k][:],
-                    lhsT=z_codes[grp, g][:, P * i : P * (i + 1)].bitcast(E5M2),
-                    lhsT_scale=z_scales[grp, g][:, P * i : P * (i + 1)],
-                    rhs=a_codes[half][:].bitcast(E4M3),
-                    rhs_scale=a_scales[half][:],
-                    start=(g == 0),
-                    stop=(g == F_PASSES - 1),
-                )
+            half = half_index(tile * P // T, g, h)
+            if g == 0:
+                y_banks[k] = psum.tile([P, NB], F32, name="bank", bufs=8)
+            nc.tensor.matmul_mx(
+                out=y_banks[k][:],
+                lhsT=z_codes[grp, g][:, P * i : P * (i + 1)].bitcast(E5M2),
+                lhsT_scale=z_scales[grp, g][:, P * i : P * (i + 1)],
+                rhs=a_codes[half][:].bitcast(E4M3),
+                rhs_scale=a_scales[half][:],
+                start=(g == 0),
+                stop=(g == F_PASSES - 1),
+            )
 
         def add_bias(k):
             tile, h = divmod(k, HALVES)
             u = tile * P // T
             if h == 0:
                 y_tiles[tile] = work.tile([P, F], F32, name="y_tile", bufs=6)
-            nc.vector.tensor_tensor(out=y_tiles[tile][:, NB * h : NB * (h + 1)], in0=y_banks[k][:], in1=b_rows[u][:, NB * h : NB * (h + 1)], op=ALU.add)
+            nc.vector.tensor_tensor(out=y_tiles[tile][:, NB * h : NB * (h + 1)], in0=y_banks[k][:], in1=b_rows[:, F * u + NB * h : F * u + NB * (h + 1)], op=ALU.add)
 
         def store(k):
             tile, h = divmod(k, HALVES)
@@ -261,16 +271,17 @@ def tile_fmllr_speaker_adaptation_s9_kernel(tc, x, lda_words, lda_scales, mean, 
                                     rhs=a_codes["w4"][:].bitcast(E4M3), rhs_scale=a_scales["w4"][:], start=True, stop=True)
 
         waiting = LOADS.split()
-        count = {"woven": 0, "quantised": 0, "adapted": 0, "added": 0, "stored": 0}
-        bank_order = list(range(18)) + [18, 20, 22, 19, 21, 23]
+        pieces = [(half, lo) for half in range(16) if half not in POOL_HALVES for lo in (0, PIECE)]
+        pool_halves = list(POOL_HALVES)
+        bank_order = list(range(16)) + [16, 18, 20, 22, 17, 19, 21, 23]
+        adapted, added, stored = [], [], []
 
         def loads():
             while waiting:
                 item = waiting[0]
                 if item[0] == "a":
                     old = 2 * int(item[1]) + int(item[2]) - RAW_A_BUFS
-                    done = [half_of(n)[:2] for n in range(count["woven"] // 2)]
-                    if old >= 0 and done.count(divmod(old, 2)) < 2:
+                    if old >= 0 and [half_of(n)[:2] for n in woven].count(divmod(old, 2)) < 2:
                         return
                     load_a(int(item[1]), int(item[2]))
                 elif item[0] == "x":
@@ -284,30 +295,42 @@ def tile_fmllr_speaker_adaptation_s9_kernel(tc, x, lda_words, lda_scales, mean, 
                 elif item == "s":
                     load_l_scales()
                 else:
-                    load_b(int(item[1]))
+                    load_b()
                 waiting.remove(item)
 
         def weave_next(engine_copy):
-            weave_a(count["woven"], engine_copy)
-            count["woven"] = count["woven"] + 1
-            loads()
+            if pieces:
+                half, lo = pieces[0]
+                pieces.remove(pieces[0])
+                weave_a(half, lo, lo + PIECE, engine_copy)
+                loads()
 
-        def quantise_until(pieces):
-            while count["quantised"] < pieces // 2:
-                quant_a(count["quantised"])
-                count["quantised"] = count["quantised"] + 1
+        def quantise(halves):
+            for half in halves:
+                if half not in a_codes:
+                    quant_a(half)
 
         def adapt_next():
-            adapt(bank_order[count["adapted"]])
-            count["adapted"] = count["adapted"] + 1
+            k = bank_order[len(adapted)]
+            tile, h = divmod(k, HALVES)
+            quantise([half_index(tile * P // T, g, h) for g in range(F_PASSES)])
+            for g in range(F_PASSES):
+                adapt(k, g)
+            adapted.append(k)
 
-        def add_until(n):
-            while count["added"] < n:
-                add_bias(bank_order[count["added"]])
-                count["added"] = count["added"] + 1
-            while not waiting and count["stored"] < count["added"]:
-                store(bank_order[count["stored"]])
-                count["stored"] = count["stored"] + 1
+        def add_next(n):
+            for k in adapted[len(added) : len(added) + n]:
+                add_bias(k)
+                added.append(k)
+                store(k)
+
+        def burst():
+            quantise([half for half in woven if half in POOL_HALVES])
+            half = pool_halves[0]
+            pool_halves.remove(half)
+            weave_a(half, 0, POOL_COLUMNS, pool_copy)
+            weave_a(half, POOL_COLUMNS, NB, nc.scalar.copy)
+            add_next(BURST)
 
         def turn_pair(pair):
             for c in range(D_PASSES):
@@ -316,12 +339,13 @@ def tile_fmllr_speaker_adaptation_s9_kernel(tc, x, lda_words, lda_scales, mean, 
             loads()
 
         make_identity(nc, ident[:])
-        loads()
         warm_operands()
-        warm(WARM_PASSES)
+        loads()
+        warm(WARM_FIRST)
         sort_stats()
         turn_stats()
         turn_pair(0)
+        warm(WARM_AGAIN)
         turn_pair(1)
         sort_l_scales()
         sort_l(0)
@@ -329,17 +353,15 @@ def tile_fmllr_speaker_adaptation_s9_kernel(tc, x, lda_words, lda_scales, mean, 
             quant_x(0, c)
 
         for slot in range(24):
-            woven = count["woven"]
+            ready = [half for half in woven if half not in POOL_HALVES]
             project(slot)
-            if slot == 2:
+            if slot == 1:
                 sort_l(1)
-            normalise(slot)
-            if slot >= SCALAR_WEAVES_FROM and slot - 1 not in TURN_SLOTS:
+            if slot > 0 and slot % 4 == 0 or slot >= ADAPT_FROM + 2:
                 weave_next(nc.scalar.copy)
             if slot > 4 and slot % 4 == 1:
-                weave_z(*divmod(slot // 4 - 1, 2))
-            add_until(count["adapted"] - 1)
-            quantise_until(woven)
+                weave_z(*divmod(slot // 4 - 1, 2), nc.vector.tensor_copy)
+            quantise(ready)
             if slot < VECTOR_WEAVES_UNTIL:
                 weave_next(nc.vector.tensor_copy)
             if slot > 4 and slot % 4 == 1:
@@ -347,22 +369,26 @@ def tile_fmllr_speaker_adaptation_s9_kernel(tc, x, lda_words, lda_scales, mean, 
             if slot - 1 in TURN_SLOTS[1::2]:
                 for c in range(D_PASSES):
                     quant_x(slot // 8 + 1, c)
-            for k in range((slot >= ADAPT_FROM) + (slot >= ADAPT_TWICE_FROM)):
+            normalise(slot)
+            if len(adapted) - len(added) == BURST:
+                burst()
+            if slot >= ADAPT_FROM:
+                adapt_next()
                 adapt_next()
             if slot in TURN_SLOTS:
                 turn_pair(2 + TURN_SLOTS.index(slot))
 
-        weave_z(2, 1)
-        quantise_until(count["woven"])
-        add_until(count["added"] + 1)
+        early = bank_order[16 : 16 + BURST]
+        weave_z(2, 1, nc.scalar.copy)
+        burst()
+        for k in early:
+            adapt(k, 0)
         quant_z(2, 1)
-        add_until(count["adapted"])
-        while count["adapted"] < 24:
-            tile, h = divmod(bank_order[count["adapted"]], HALVES)
-            need = 2 * (4 * (tile * P // T) + 2 * h + 2)
-            while count["woven"] < need:
-                weave_next(nc.scalar.copy)
-            quantise_until(need)
+        for k in early:
+            adapt(k, 1)
+            adapted.append(k)
+        burst()
+        for k in range(BURST):
             adapt_next()
-            add_until(count["adapted"] - 1)
-        add_until(24)
+            quantise(woven)
+            add_next(1)

@@ -166,7 +166,7 @@ def tile_fmllr_speaker_adaptation_s9_kernel(tc, x, lda_words, lda_scales, mean, 
             )
 
         def pool_copy(out, in_):
-            nc.gpsimd.tensor_scalar(out=out, in0=in_, scalar1=1.0, scalar2=0.0, op0=ALU.mult, op1=ALU.add)
+            nc.gpsimd.tensor_scalar(out=out.rearrange("p c t i -> p c i t"), in0=in_.rearrange("p c t i -> p c i t"), scalar1=1.0, scalar2=0.0, op0=ALU.mult, op1=ALU.add)
 
         def weave_a(half, lo, hi, engine_copy):
             u, g, h = half_of(half)

@@ -33,13 +33,13 @@ PIECES = U * F_PASSES * (F // PIECE)
 
 WARM_FIRST, WARM_AGAIN = 3, 2
 TURN_SLOTS = (3, 5, 8, 10)
-VECTOR_WEAVES_UNTIL = 13
-ADAPT_FROM = 16
+VECTOR_WEAVES_UNTIL = 14
+ADAPT_SLOTS = (17, 18, 19)
 BURST = 4
-POOL_COLUMNS = 384
+POOL_COLUMNS = 352
 POOL_HALVES = (9, 11, 13, 14, 15)
 RAW_A_BUFS = 5
-LOADS = "m x0 x1 s l0 a00 l1 x2 a01 x3 a10 x4 a11 x5 a20 b a21 a30 a31"
+LOADS = "m x0 x1 s l0 a00 l1 x2 a01 x3 a10 x4 x5 a11 a20 a21 b0 a30 a31 b1"
 
 
 def half_of(n):
@@ -75,7 +75,7 @@ def tile_fmllr_speaker_adaptation_s9_kernel(tc, x, lda_words, lda_scales, mean, 
         z_raw, z_grouped, z_codes, z_scales = {}, {}, {}, {}
         woven = []
         y_tiles, x_banks, h_banks, y_banks = {}, {}, {}, {}
-        b_rows = keep.tile([P, U * F], BF16, name="b_rows")
+        b_rows = {}
 
         def load_x(pair):
             x_raw[pair] = work.tile([P, 2, D], BF16, name="x_raw", bufs=4)
@@ -105,8 +105,9 @@ def tile_fmllr_speaker_adaptation_s9_kernel(tc, x, lda_words, lda_scales, mean, 
             for i in range(4):
                 nc.sync.dma_start(out=a_raw[u, g][i:P:4, :, :], in_=rows[i])
 
-        def load_b():
-            nc.sync.dma_start(out=b_rows[:], in_=b.rearrange("u f -> (u f)").partition_broadcast(P))
+        def load_b(part):
+            b_rows[part] = keep.tile([P, 2 * F], BF16, name="b_rows%d" % part)
+            nc.sync.dma_start(out=b_rows[part][:], in_=b[2 * part : 2 * part + 2, :].rearrange("u f -> (u f)").partition_broadcast(P))
 
         def sort_l(g):
             l_codes[g] = keep.tile([P, D_PASSES, F], U8, name="l_codes%d" % g, align_bytes=64)
@@ -247,7 +248,7 @@ def tile_fmllr_speaker_adaptation_s9_kernel(tc, x, lda_words, lda_scales, mean, 
             u = tile * P // T
             if h == 0:
                 y_tiles[tile] = work.tile([P, F], F32, name="y_tile", bufs=6)
-            nc.vector.tensor_tensor(out=y_tiles[tile][:, NB * h : NB * (h + 1)], in0=y_banks[k][:], in1=b_rows[:, F * u + NB * h : F * u + NB * (h + 1)], op=ALU.add)
+            nc.vector.tensor_tensor(out=y_tiles[tile][:, NB * h : NB * (h + 1)], in0=y_banks[k][:], in1=b_rows[u // 2][:, F * (u % 2) + NB * h : F * (u % 2) + NB * (h + 1)], op=ALU.add)
 
         def store(k):
             tile, h = divmod(k, HALVES)
@@ -295,7 +296,7 @@ def tile_fmllr_speaker_adaptation_s9_kernel(tc, x, lda_words, lda_scales, mean, 
                 elif item == "s":
                     load_l_scales()
                 else:
-                    load_b()
+                    load_b(int(item[1]))
                 waiting.remove(item)
 
         def weave_next(engine_copy):
@@ -357,7 +358,7 @@ def tile_fmllr_speaker_adaptation_s9_kernel(tc, x, lda_words, lda_scales, mean, 
             project(slot)
             if slot == 1:
                 sort_l(1)
-            if slot > 0 and slot % 4 == 0 or slot >= ADAPT_FROM + 2:
+            if slot > 0 and slot % 4 == 0 or slot >= 16:
                 weave_next(nc.scalar.copy)
             if slot > 4 and slot % 4 == 1:
                 weave_z(*divmod(slot // 4 - 1, 2), nc.vector.tensor_copy)
@@ -372,13 +373,15 @@ def tile_fmllr_speaker_adaptation_s9_kernel(tc, x, lda_words, lda_scales, mean, 
             normalise(slot)
             if len(adapted) - len(added) == BURST:
                 burst()
-            if slot >= ADAPT_FROM:
-                adapt_next()
-                adapt_next()
+            if slot in ADAPT_SLOTS:
+                for k in range(BURST):
+                    adapt_next()
             if slot in TURN_SLOTS:
                 turn_pair(2 + TURN_SLOTS.index(slot))
 
         early = bank_order[16 : 16 + BURST]
+        for k in range(BURST):
+            adapt_next()
         weave_z(2, 1, nc.scalar.copy)
         burst()
         for k in early:

@@ -31,7 +31,6 @@ PIECE = 256
 PIECES = U * F_PASSES * (F // PIECE)
 
 
-WARM_FIRST, WARM_AGAIN = 3, 2
 TURN_SLOTS = (3, 5, 8, 10)
 VECTOR_WEAVES_UNTIL = 14
 ADAPT_SLOTS = (17, 18, 19)
@@ -101,9 +100,9 @@ def tile_fmllr_speaker_adaptation_s9_kernel(tc, x, lda_words, lda_scales, mean, 
 
         def load_a(u, g):
             a_raw[u, g] = work.tile([P, PACK, F], BF16, name="a_raw", bufs=RAW_A_BUFS)
-            rows = a[u, KP * g : KP * (g + 1), :].rearrange("(j t i) n -> i j t n", t=PACK, i=4)
-            for i in range(4):
-                nc.sync.dma_start(out=a_raw[u, g][i:P:4, :, :], in_=rows[i])
+            rows = a[u, KP * g : KP * (g + 1), :].rearrange("(j t i) n -> t j i n", t=PACK, i=4)
+            for t in range(PACK):
+                nc.sync.dma_start(out=a_raw[u, g][:, t, :], in_=rows[t])
 
         def load_b(part):
             b_rows[part] = keep.tile([P, 2 * F], BF16, name="b_rows%d" % part)
@@ -257,20 +256,6 @@ def tile_fmllr_speaker_adaptation_s9_kernel(tc, x, lda_words, lda_scales, mean, 
             elif h == 1:
                 nc.sync.dma_start(out=out_rows[P * tile : P * (tile + 1), :], in_=y_tiles[tile][:])
 
-        def warm_operands():
-            zeros = keep.tile([P, NB * PACK], BF16, name="zeros", align_bytes=64)
-            nc.vector.memset(zeros[:].bitcast(I32), 0)
-            for name, cols, fmt in (("w4", NB, E4M3), ("w5", P, E5M2)):
-                a_codes[name] = keep.tile([P, cols], U32, name=name + "c", align_bytes=64)
-                a_scales[name] = keep.tile([P, cols], U8, name=name + "s", align_bytes=64)
-                nc.vector.quantize_mx(out=a_codes[name][:].bitcast(fmt), scales=a_scales[name][:], in_=zeros[:, : cols * PACK])
-
-        def warm(n):
-            bank = psum.tile([P, NB], F32, name="bank", bufs=8)
-            for k in range(n):
-                nc.tensor.matmul_mx(out=bank[:], lhsT=a_codes["w5"][:].bitcast(E5M2), lhsT_scale=a_scales["w5"][:],
-                                    rhs=a_codes["w4"][:].bitcast(E4M3), rhs_scale=a_scales["w4"][:], start=True, stop=True)
-
         waiting = LOADS.split()
         pieces = [(half, lo) for half in range(16) if half not in POOL_HALVES for lo in (0, PIECE)]
         pool_halves = list(POOL_HALVES)
@@ -340,13 +325,10 @@ def tile_fmllr_speaker_adaptation_s9_kernel(tc, x, lda_words, lda_scales, mean, 
             loads()
 
         make_identity(nc, ident[:])
-        warm_operands()
         loads()
-        warm(WARM_FIRST)
         sort_stats()
         turn_stats()
         turn_pair(0)
-        warm(WARM_AGAIN)
         turn_pair(1)
         sort_l_scales()
         sort_l(0)

from contextlib import ExitStack

import concourse.mybir as mybir
from concourse.masks import make_identity

U, T, D, F = 4, 384, 1536, 1024
FLOPS = 2 * U * T * D * F + 2 * U * T * F * F

F32 = mybir.dt.float32
BF16 = mybir.dt.bfloat16
I32 = mybir.dt.int32
U32 = mybir.dt.uint32
U8 = mybir.dt.uint8
E4M3 = mybir.dt.float8_e4m3fn_x4
E5M2 = mybir.dt.float8_e5m2_x4
E2M1 = mybir.dt.float4_e2m1fn_x4
ALU = mybir.AluOpType
ACT = mybir.ActivationFunctionType

P = 128
PACK = 4
KP = P * PACK
NB = 512
D_PASSES = D // KP
F_PASSES = F // KP
TOKENS = U * T
GROUPS = TOKENS // NB
TILES = TOKENS // P
HALVES = F // NB
PIECE = 256
PIECES = U * F_PASSES * (F // PIECE)


TURN_SLOTS = (3, 5, 8, 10)
VECTOR_WEAVES_UNTIL = 14
ADAPT_SLOTS = (17, 18, 19)
BURST = 4
POOL_COLUMNS = 352
POOL_HALVES = (9, 11, 13, 14, 15)
RAW_A_BUFS = 5
LOADS = "m x0 x1 s l0 a00 l1 x2 a01 x3 a10 x4 x5 a11 a20 a21 b0 a30 a31 b1"


def half_of(n):
    u, rest = divmod(n, 4)
    first, second = divmod(rest, 2)
    return (u, first, second) if u < 2 else (u, second, first)


def half_index(u, g, h):
    return 4 * u + (2 * g + h if u < 2 else 2 * h + g)


def tile_fmllr_speaker_adaptation_s9_kernel(tc, x, lda_words, lda_scales, mean, inv_std, a, b, out):
    nc = tc.nc
    out_rows = out.rearrange("u t f -> (u t) f")

    with ExitStack() as ctx:
        keep = ctx.enter_context(tc.tile_pool(name="keep", bufs=1))
        work = ctx.enter_context(tc.tile_pool(name="work", bufs=2))
        psum = ctx.enter_context(tc.psum_pool(name="psum", bufs=1))
        ctx.enter_context(tc.manual_schedule())

        ident = keep.tile([P, P], F32, name="ident")
        stat_rows = keep.tile([16, KP], BF16, name="stat_rows")
        stat_sorted = keep.tile([P, PACK, P], F32, name="stat_sorted")
        stat_cols = keep.tile([P, PACK, 16], F32, name="stat_cols")
        shift = keep.tile([P, PACK, 8], F32, name="shift")
        l_scales_raw = keep.tile([P, D_PASSES * F], U8, name="l_scales_raw", align_bytes=64)
        l_scales = keep.tile([P, D_PASSES * F], U8, name="l_scales", align_bytes=64)
        l_raw, l_codes = {}, {}
        x_raw, x_grouped, x_codes, x_scales = {}, {}, {}, {}
        a_raw, a_grouped, a_codes, a_scales = {}, {}, {}, {}
        z_raw, z_grouped, z_codes, z_scales = {}, {}, {}, {}
        woven = []
        y_tiles, x_banks, h_banks, y_banks = {}, {}, {}, {}
        b_rows = {}

        def load_x(pair):
            x_raw[pair] = work.tile([P, 2, D], BF16, name="x_raw", bufs=4)
            nc.sync.dma_start(out=x_raw[pair][:], in_=x[2 * P * pair : 2 * P * (pair + 1), :].rearrange("(i p) d -> p i d", p=P))

        def load_l(g):
            l_raw[g] = keep.tile([P, D_PASSES, F], U8, name="l_raw%d" % g, align_bytes=64)
            words = lda_words.bitcast(I32).rearrange("c p (g w) -> g p c w", g=F_PASSES)
            nc.sync.dma_start(out=l_raw[g][:].bitcast(I32), in_=words[g])

        def load_l_scales():
            nc.vector.memset(l_scales_raw[:].bitcast(I32), 0)
            rows = lda_scales.bitcast(I32)
            for q in range(4):
                nc.sync.dma_start(
                    out=l_scales_raw[32 * q : 32 * q + 4, :].bitcast(I32).rearrange("r (c w) -> r c w", c=D_PASSES),
                    in_=rows[:, 4 * q : 4 * q + 4, :].rearrange("c r w -> r c w"),
                )

        def load_stats():
            nc.sync.dma_start(out=stat_rows[0:8, :], in_=mean.rearrange("u (g k) -> (u g) k", k=KP))
            nc.sync.dma_start(out=stat_rows[8:16, :], in_=inv_std.rearrange("u (g k) -> (u g) k", k=KP))

        def load_a(u, g):
            a_raw[u, g] = work.tile([P, PACK, F], BF16, name="a_raw", bufs=RAW_A_BUFS)
            rows = a[u, KP * g : KP * (g + 1), :].rearrange("(j t i) n -> t j i n", t=PACK, i=4)
            for t in range(PACK):
                nc.sync.dma_start(out=a_raw[u, g][:, t, :], in_=rows[t])

        def load_b(part):
            b_rows[part] = keep.tile([P, 2 * F], BF16, name="b_rows%d" % part)
            nc.sync.dma_start(out=b_rows[part][:], in_=b[2 * part : 2 * part + 2, :].rearrange("u f -> (u f)").partition_broadcast(P))

        def sort_l(g):
            l_codes[g] = keep.tile([P, D_PASSES, F], U8, name="l_codes%d" % g, align_bytes=64)
            nc.vector.tensor_copy(
                out=l_codes[g][:].bitcast(I32).rearrange("p c (t j w) -> p c t j w", t=PACK, w=2),
                in_=l_raw[g][:].bitcast(I32).rearrange("p c (j t w) -> p c t j w", t=PACK, w=2),
            )

        def sort_l_scales():
            nc.vector.tensor_copy(
                out=l_scales[:].bitcast(I32).rearrange("p (m t j) -> p m t j", t=PACK, j=32),
                in_=l_scales_raw[:].bitcast(I32).rearrange("p (m j t) -> p m t j", t=PACK, j=32),
            )

        def sort_stats():
            nc.vector.memset(stat_sorted[:], 0.0)
            nc.vector.tensor_copy(
                out=stat_sorted[0:16, :, :].rearrange("r t (j i) -> r t j i", i=4),
                in_=stat_rows[:].rearrange("r (j t i) -> r t j i", t=PACK, i=4),
            )

        def turn_stats():
            bank = psum.tile([P, PACK, P], F32, name="bank", bufs=8)
            for t in range(PACK):
                nc.tensor.transpose(bank[:, t, :], stat_sorted[:, t, :], ident[:])
            nc.scalar.activation(out=stat_cols[:], in_=bank[:, :, 0:16], func=ACT.Identity)
            nc.vector.scalar_tensor_tensor(
                out=shift[:], in0=stat_cols[:, :, 0:8], scalar=-1.0, in1=stat_cols[:, :, 8:16], op0=ALU.mult, op1=ALU.mult
            )

        def turn_x(pair, c):
            x_banks[pair, c] = psum.tile([P, 2, 2, P], F32, name="bank", bufs=8)
            for i in range(2):
                words = x_raw[pair][:, i, :].bitcast(F32)
                for e in range(2):
                    nc.tensor.transpose(x_banks[pair, c][:, i, e, :], words[:, 256 * c + e : 256 * (c + 1) : 2], ident[:])

        def copy_x(pair, c):
            grp, half = divmod(pair, 2)
            if half == 0:
                x_grouped[grp, c] = work.tile([P, NB * PACK], BF16, name="x_grouped", bufs=4, align_bytes=64)
            dst = x_grouped[grp, c][:, half * 2 * P * PACK : (half + 1) * 2 * P * PACK].bitcast(F32)
            nc.scalar.copy(
                out=dst.rearrange("p (i r e) -> p i r e", i=2, e=2),
                in_=x_banks[pair, c][:].rearrange("p i e r -> p i r e"),
            )

        def quant_x(grp, c):
            x_codes[grp, c] = work.tile([P, NB], U32, name="x_codes", bufs=6, align_bytes=64)
            x_scales[grp, c] = work.tile([P, NB], U8, name="x_scales", bufs=6, align_bytes=64)
            nc.vector.quantize_mx(out=x_codes[grp, c][:].bitcast(E4M3), scales=x_scales[grp, c][:], in_=x_grouped[grp, c][:])

        def weave(engine_copy, dst, src):
            engine_copy(
                out=dst.rearrange("p (c i t) -> p c t i", i=4, t=PACK),
                in_=src.rearrange("p t (c i) -> p c t i", i=4),
            )

        def pool_copy(out, in_):
            nc.gpsimd.tensor_scalar(out=out.rearrange("p c t i -> p c i t"), in0=in_.rearrange("p c t i -> p c i t"), scalar1=1.0, scalar2=0.0, op0=ALU.mult, op1=ALU.add)

        def weave_a(half, lo, hi, engine_copy):
            u, g, h = half_of(half)
            if lo == 0 and half in POOL_HALVES:
                a_grouped[half] = work.tile([P, NB * PACK], BF16, name="gated", bufs=1, align_bytes=64)
            elif lo == 0:
                a_grouped[half] = work.tile([P, NB * PACK], BF16, name="a_grouped", bufs=4, align_bytes=64)
            weave(engine_copy, a_grouped[half][:, PACK * lo : PACK * hi], a_raw[u, g][:, :, NB * h + lo : NB * h + hi])
            if hi == NB:
                woven.append(half)

        def quant_a(half):
            a_codes[half] = work.tile([P, NB], U32, name="a_codes", bufs=12, align_bytes=64)
            a_scales[half] = work.tile([P, NB], U8, name="a_scales", bufs=12, align_bytes=64)
            nc.vector.quantize_mx(out=a_codes[half][:].bitcast(E4M3), scales=a_scales[half][:], in_=a_grouped[half][:])

        def project(slot):
            grp, g, t = slot // 8, slot // 4 % 2, slot % 4
            h_banks[slot] = psum.tile([P, NB], F32, name="bank", bufs=8)
            m = (g * PACK + t) * P
            for c in range(D_PASSES):
                nc.tensor.matmul_mx(
                    out=h_banks[slot][:],
                    lhsT=l_codes[g][:, c, 2 * P * t : 2 * P * (t + 1)].bitcast(E2M1),
                    lhsT_scale=l_scales[:, c * F + m : c * F + m + P],
                    rhs=x_codes[grp, c][:].bitcast(E4M3),
                    rhs_scale=x_scales[grp, c][:],
                    start=(c == 0),
                    stop=(c == D_PASSES - 1),
                )

        def normalise(slot):
            grp, g, t = slot // 8, slot // 4 % 2, slot % 4
            if t == 0:
                z_raw[grp, g] = work.tile([P, PACK, NB], BF16, name="z_raw", bufs=2)
            first = NB * grp
            cut = (first // T + 1) * T
            for lo, hi in ((first, cut), (cut, first + NB)):
                row = (lo // T) * F_PASSES + g
                nc.scalar.activation(
                    out=z_raw[grp, g][:, t, lo - first : hi - first],
                    in_=h_banks[slot][:, lo - first : hi - first],
                    func=ACT.Identity,
                    bias=shift[:, t, row : row + 1],
                    scale=stat_cols[:, t, 8 + row : 8 + row + 1],
                )

        def weave_z(grp, g, engine_copy):
            if (grp, g) == (1, 1):
                z_grouped[grp, g] = work.tile([P, NB * PACK], BF16, name="gated", bufs=1, align_bytes=64)
            else:
                z_grouped[grp, g] = work.tile([P, NB * PACK], BF16, name="z_grouped", bufs=2, align_bytes=64)
            weave(engine_copy, z_grouped[grp, g][:], z_raw[grp, g][:])

        def quant_z(grp, g):
            z_codes[grp, g] = work.tile([P, NB], U32, name="z_codes", bufs=4, align_bytes=64)
            z_scales[grp, g] = work.tile([P, NB], U8, name="z_scales", bufs=4, align_bytes=64)
            nc.vector.quantize_mx(out=z_codes[grp, g][:].bitcast(E5M2), scales=z_scales[grp, g][:], in_=z_grouped[grp, g][:])

        def adapt(k, g):
            tile, h = divmod(k, HALVES)
            grp, i = divmod(tile, 4)
            half = half_index(tile * P // T, g, h)
            if g == 0:
                y_banks[k] = psum.tile([P, NB], F32, name="bank", bufs=8)
            nc.tensor.matmul_mx(
                out=y_banks[k][:],
                lhsT=z_codes[grp, g][:, P * i : P * (i + 1)].bitcast(E5M2),
                lhsT_scale=z_scales[grp, g][:, P * i : P * (i + 1)],
                rhs=a_codes[half][:].bitcast(E4M3),
                rhs_scale=a_scales[half][:],
                start=(g == 0),
                stop=(g == F_PASSES - 1),
            )

        def add_bias(k):
            tile, h = divmod(k, HALVES)
            u = tile * P // T
            if h == 0:
                y_tiles[tile] = work.tile([P, F], F32, name="y_tile", bufs=6)
            nc.vector.tensor_tensor(out=y_tiles[tile][:, NB * h : NB * (h + 1)], in0=y_banks[k][:], in1=b_rows[u // 2][:, F * (u % 2) + NB * h : F * (u % 2) + NB * (h + 1)], op=ALU.add)

        def store(k):
            tile, h = divmod(k, HALVES)
            if tile >= 8:
                nc.sync.dma_start(out=out_rows[P * tile : P * (tile + 1), NB * h : NB * (h + 1)], in_=y_tiles[tile][:, NB * h : NB * (h + 1)])
            elif h == 1:
                nc.sync.dma_start(out=out_rows[P * tile : P * (tile + 1), :], in_=y_tiles[tile][:])

        waiting = LOADS.split()
        pieces = [(half, lo) for half in range(16) if half not in POOL_HALVES for lo in (0, PIECE)]
        pool_halves = list(POOL_HALVES)
        bank_order = list(range(16)) + [16, 18, 20, 22, 17, 19, 21, 23]
        adapted, added, stored = [], [], []

        def loads():
            while waiting:
                item = waiting[0]
                if item[0] == "a":
                    old = 2 * int(item[1]) + int(item[2]) - RAW_A_BUFS
                    if old >= 0 and [half_of(n)[:2] for n in woven].count(divmod(old, 2)) < 2:
                        return
                    load_a(int(item[1]), int(item[2]))
                elif item[0] == "x":
                    if int(item[1]) >= 4 and (int(item[1]) - 4, 2) not in x_banks:
                        return
                    load_x(int(item[1]))
                elif item[0] == "l":
                    load_l(int(item[1]))
                elif item == "m":
                    load_stats()
                elif item == "s":
                    load_l_scales()
                else:
                    load_b(int(item[1]))
                waiting.remove(item)

        def weave_next(engine_copy):
            if pieces:
                half, lo = pieces[0]
                pieces.remove(pieces[0])
                weave_a(half, lo, lo + PIECE, engine_copy)
                loads()

        def quantise(halves):
            for half in halves:
                if half not in a_codes:
                    quant_a(half)

        def adapt_next():
            k = bank_order[len(adapted)]
            tile, h = divmod(k, HALVES)
            quantise([half_index(tile * P // T, g, h) for g in range(F_PASSES)])
            for g in range(F_PASSES):
                adapt(k, g)
            adapted.append(k)

        def add_next(n):
            for k in adapted[len(added) : len(added) + n]:
                add_bias(k)
                added.append(k)
                store(k)

        def burst():
            quantise([half for half in woven if half in POOL_HALVES])
            half = pool_halves[0]
            pool_halves.remove(half)
            weave_a(half, 0, POOL_COLUMNS, pool_copy)
            weave_a(half, POOL_COLUMNS, NB, nc.scalar.copy)
            add_next(BURST)

        def turn_pair(pair):
            for c in range(D_PASSES):
                turn_x(pair, c)
                copy_x(pair, c)
            loads()

        make_identity(nc, ident[:])
        loads()
        sort_stats()
        turn_stats()
        turn_pair(0)
        turn_pair(1)
        sort_l_scales()
        sort_l(0)
        for c in range(D_PASSES):
            quant_x(0, c)

        for slot in range(24):
            ready = [half for half in woven if half not in POOL_HALVES]
            project(slot)
            if slot == 1:
                sort_l(1)
            if slot > 0 and slot % 4 == 0 or slot >= 16:
                weave_next(nc.scalar.copy)
            if slot > 4 and slot % 4 == 1:
                weave_z(*divmod(slot // 4 - 1, 2), nc.vector.tensor_copy)
            quantise(ready)
            if slot < VECTOR_WEAVES_UNTIL:
                weave_next(nc.vector.tensor_copy)
            if slot > 4 and slot % 4 == 1:
                quant_z(*divmod(slot // 4 - 1, 2))
            if slot - 1 in TURN_SLOTS[1::2]:
                for c in range(D_PASSES):
                    quant_x(slot // 8 + 1, c)
            normalise(slot)
            if len(adapted) - len(added) == BURST:
                burst()
            if slot in ADAPT_SLOTS:
                for k in range(BURST):
                    adapt_next()
            if slot in TURN_SLOTS:
                turn_pair(2 + TURN_SLOTS.index(slot))

        early = bank_order[16 : 16 + BURST]
        for k in range(BURST):
            adapt_next()
        weave_z(2, 1, nc.scalar.copy)
        burst()
        for k in early:
            adapt(k, 0)
        quant_z(2, 1)
        for k in early:
            adapt(k, 1)
            adapted.append(k)
        burst()
        for k in range(BURST):
            adapt_next()
            quantise(woven)
            add_next(1)
